import numpy as np
import ml_dtypes


def mxq(x, axis, fmt="e4m3"):
    dtype, down = {"e4m3": (ml_dtypes.float8_e4m3fn, 7), "e5m2": (ml_dtypes.float8_e5m2, 14)}[fmt]
    v = np.moveaxis(np.asarray(x, np.float32).astype(ml_dtypes.bfloat16).astype(np.float64), axis, -1)
    blocks = v.reshape(v.shape[:-1] + (-1, 32))
    amax = np.abs(blocks).max(-1, keepdims=True)
    byte = np.maximum(np.where(amax > 0, np.frexp(amax)[1] - 1 + 127, 0) - down, 1)
    scale = np.exp2(byte - 127.0)
    codes = (blocks / scale).astype(np.float32).astype(dtype).astype(np.float64)
    return np.moveaxis((codes * scale).reshape(v.shape), -1, axis)


WIDE = False


def mx_kscale(k):
    if not WIDE:
        return np.ones(k)
    levels = np.array([10, -10, 5, -5, 0])
    if k % 512:
        return np.exp2(np.random.permutation(np.resize(levels, k // 32))).repeat(32)
    a = np.empty((k // 512, 16))
    for p in range(k // 512):
        a[p, :8] = np.random.permutation(np.resize(levels, 8))
        for g in range(8):
            far = levels[np.abs(levels - a[p, g]) >= 10]
            a[p, g + 8] = far[np.random.randint(len(far))]
    return np.exp2(a.ravel()).repeat(32)


def f64(x):
    return np.asarray(x).astype(np.float64)


def striped(idx):
    return np.tile(idx.reshape(-1, 16).T, (8, 1)).astype(np.uint16)


def unstriped(offs):
    return offs[:16].T.reshape(-1).astype(np.int64)


E2M1 = np.array([0.0, 0.5, 1.0, 1.5, 2.0, 3.0, 4.0, 6.0, -0.0, -0.5, -1.0, -1.5, -2.0, -3.0, -4.0, -6.0])


def pack_weight(w, fmt):
    k, n = w.shape
    w = f64(np.asarray(w, np.float32).astype(ml_dtypes.bfloat16)).reshape(k // 32, 32, n)
    amax = np.abs(w).max(1)
    if fmt == "e4m3":
        byte = np.frexp(amax)[1] - 1 + 127 - 7
    else:
        mant, ex = np.frexp(amax / 6.0)
        byte = np.where(mant > 0.5, ex, ex - 1) + 127
    byte = np.clip(np.where(amax > 0, byte, 1), 1, 254)
    scaled = (w * np.exp2(127.0 - byte)[:, None, :]).reshape(k, n).astype(np.float32)
    by_word = np.ascontiguousarray(scaled.reshape(k // 512, 128, 4, n).transpose(0, 1, 3, 2))
    if fmt == "e4m3":
        words = by_word.astype(ml_dtypes.float8_e4m3fn).view(np.uint8)
    else:
        c = by_word.astype(ml_dtypes.float4_e2m1fn).view(np.uint8) & 0xF
        words = (c[..., 0::2] | (c[..., 1::2] << 4)).reshape(k // 512, 128, 2 * n)
    return np.ascontiguousarray(words), np.ascontiguousarray(byte.astype(np.uint8).reshape(k // 512, 16, n))


def unpack_weight(words, scales, fmt):
    g, _, n = scales.shape
    words = np.ascontiguousarray(words).reshape(g, 128, n, -1)
    if fmt == "e4m3":
        vals = words.view(ml_dtypes.float8_e4m3fn).astype(np.float64)
    else:
        nib = np.empty((g, 128, n, 4), np.uint8)
        nib[..., 0::2] = words & 0xF
        nib[..., 1::2] = words >> 4
        vals = E2M1[nib]
    vals = vals * np.repeat(np.exp2(scales.astype(np.float64) - 127.0), 8, axis=1)[..., None]
    return vals.transpose(0, 1, 3, 2).reshape(g * 512, n)


def sigmoid(v):
    return 1.0 / (1.0 + np.exp(-np.maximum(v, -700.0)))


K, T, E, C, H, N = 1536, 1024, 4, 128, 512, 128


def by_expert(wq, xq):
    return np.concatenate([wq[e].T @ xq[:, e * C:(e + 1) * C] for e in range(E)], axis=1)


def setup_inputs():
    n = np.random.standard_normal
    s = mx_kscale(K)[:, None]
    u = mx_kscale(H)
    x = pack_weight(n((K, T)) * s, "e4m3")
    return {
        "x_words": x[0],
        "x_scales": x[1],
        "w1": (n((E, K, H)) / np.sqrt(K) / s[None]).astype(np.float32),
        "w3": (n((E, K, H)) / np.sqrt(K) / s[None] * u[None, None, :]).astype(np.float32),
        "w2": (n((E, H, N)) / np.sqrt(H) / u[None, :, None]).astype(np.float32),
        "gate": np.tile(np.random.uniform(0.2, 1.0, E * C), (N, 1)).astype(np.float32),
        "offs": striped(np.random.permutation(T)[:E * C]),
    }


def reference(x_words, x_scales, w1, w3, w2, gate, offs):
    idx = unstriped(offs)
    xq = unpack_weight(x_words, x_scales, "e4m3")[:, idx]
    h = sigmoid(by_expert(mxq(f64(w1), 1, "e4m3"), xq))
    h = h * by_expert(mxq(f64(w3), 1, "e4m3"), xq)
    y = by_expert(mxq(f64(w2), 1, "e4m3"), mxq(h, 0, "e4m3"))
    out = np.zeros((N, T))
    out[:, idx] = f64(gate) * y
    return out

@@ -1,0 +1,252 @@
+from contextlib import ExitStack
+
+import concourse.mybir as mybir
+from concourse.masks import make_identity
+
+K, T, E, C, H, N = 1536, 1024, 4, 128, 512, 128
+S = E * C
+FLOPS = 2 * S * (2 * K * H + H * N)
+BYTES = K * T + K * T // 32 + 4 * E * (2 * K * H + H * N) + 4 * S + 2 * 128 * S // 16 + 4 * N * T
+
+F32 = mybir.dt.float32
+BF16 = mybir.dt.bfloat16
+I32 = mybir.dt.int32
+U32 = mybir.dt.uint32
+U16 = mybir.dt.uint16
+U8 = mybir.dt.uint8
+FP8X4 = mybir.dt.float8_e4m3fn_x4
+MULT = mybir.AluOpType.mult
+SIGMOID = mybir.ActivationFunctionType.Sigmoid
+
+P = 128
+PACK = 4
+K_PASS = P * PACK
+PASSES = K // K_PASS
+LIST_COLS = C // 16
+SCALAR_EIGHTHS = 5
+SCALAR_COLS = H * SCALAR_EIGHTHS // 8
+LAST_RANGES = ((0, 256), (256, 384), (384, 512))
+LOAD_AHEAD = 10
+
+
+def tile_moe_pkd_glu_sigmoid_kernel(tc, x_words, x_scales, w1, w3, w2, gate, offs, out):
+    nc = tc.nc
+    with ExitStack() as ctx:
+        keep = ctx.enter_context(tc.tile_pool(name="keep", bufs=1))
+        raw_pool = ctx.enter_context(tc.tile_pool(name="raw", bufs=LOAD_AHEAD + 2))
+        coded = ctx.enter_context(tc.tile_pool(name="coded", bufs=4))
+        tail = ctx.enter_context(tc.tile_pool(name="tail", bufs=2))
+        sums = ctx.enter_context(tc.psum_pool(name="sums", bufs=6))
+        small = ctx.enter_context(tc.psum_pool(name="small", bufs=1))
+
+        offsets = keep.tile([P, S // 16], U16, name="offsets")
+        token_words = [keep.tile([P, T], I32, name="token_words%d" % o) for o in range(PASSES)]
+        token_scales = keep.tile([P, T], U8, name="token_scales")
+        slot_words = [keep.tile([P, S], U32, name="slot_words%d" % o, align_bytes=64) for o in range(PASSES)]
+        slot_scales = keep.tile([P, S], U8, name="slot_scales", align_bytes=64)
+        gate_rows = keep.tile([P, PACK], F32, name="gate_rows")
+        gate_wide = keep.tile([P, S], F32, name="gate_wide")
+        ident = keep.tile([P, P], F32, name="ident")
+        staging = keep.tile([P, (H + SCALAR_COLS) * PACK], BF16, name="staging", align_bytes=64)
+        result = keep.tile([N, T], F32, name="result")
+
+        nc.gpsimd.memset(token_scales[:].bitcast(I32), 0)
+        nc.gpsimd.memset(result[:], 0.0)
+        make_identity(nc, ident[:])
+
+        def load_words(o):
+            nc.sync.dma_start(token_words[o][:], x_words[o].rearrange("p t r -> p (t r)").bitcast(I32))
+
+        def load_scales():
+            for q in range(4):
+                nc.sync.dma_start(token_scales[32 * q:32 * q + 4 * PASSES, :].bitcast(I32),
+                                  x_scales[:, 4 * q:4 * q + 4, :].bitcast(I32))
+
+        def gather_words(o):
+            nc.vector.tensor_copy(slot_words[o][:], token_words[o][:].bitcast(U32).indirect(offsets[:]))
+
+        def spread_gate():
+            turned = small.tile([P, PACK, P], F32, name="turned", tag="turned")
+            for f in range(PACK):
+                nc.tensor.transpose(turned[:, f, :], gate_rows[:, f:f + 1].to_broadcast([P, P]), ident[:])
+            nc.scalar.copy(gate_wide[:].rearrange("n (p f) -> n p f", f=PACK), turned[:].rearrange("n f p -> n p f"))
+
+        pieces = []
+        for e in range(E):
+            last = e == E - 1
+            for o in range(PASSES):
+                pieces.append(("w1", e, o, 0, H))
+            if not last:
+                pieces.append(("w2", e, 0, 0, N))
+            for o in range(PASSES):
+                if last and o == PASSES - 1:
+                    pieces.extend(("w3", e, o, c0, c1) for c0, c1 in LAST_RANGES)
+                else:
+                    pieces.append(("w3", e, o, 0, H))
+            if last:
+                pieces.append(("w2", e, 0, 0, N))
+        source = {"w1": w1, "w3": w3, "w2": w2}
+        raw, rounded, codes, banks, sigs, hidden, second = {}, {}, {}, {}, {}, {}, {}
+
+        def load(piece):
+            kind, e, o, c0, c1 = piece
+            raw[piece] = raw_pool.tile([P, PACK, c1 - c0], F32, name="raw", tag="raw")
+            rows = source[kind][e, o * K_PASS:(o + 1) * K_PASS, c0:c1]
+            nc.sync.dma_start(raw[piece][:], rows.rearrange("(p j) c -> p j c", j=PACK))
+
+        def round_columns(copy, at, piece, a, b):
+            target = staging[:, at * PACK:(at + b - a) * PACK]
+            copy(target.rearrange("p (c i j) -> p c j i", i=4, j=PACK),
+                 raw[piece][:, :, a:b].rearrange("p j (c i) -> p c j i", i=4))
+            return target
+
+        def interleave(i, between):
+            piece = pieces[i]
+            width = piece[4] - piece[3]
+            by_scalar = width * SCALAR_EIGHTHS // 8
+            by_vector = width - by_scalar
+            if i % 2 == 0:
+                start = SCALAR_COLS - by_scalar
+                round_columns(nc.scalar.copy, start, piece, 0, by_scalar)
+            else:
+                start = H - by_vector
+                round_columns(nc.scalar.copy, H, piece, by_vector, width)
+            for stage, e in between:
+                stage(e)
+            if i % 2 == 0:
+                round_columns(nc.vector.tensor_copy, SCALAR_COLS, piece, by_scalar, width)
+            else:
+                round_columns(nc.vector.tensor_copy, start, piece, 0, by_vector)
+            return staging[:, start * PACK:(start + width) * PACK]
+
+        def new_codes(width, tag, pool):
+            words = pool.tile([P, width], U32, name="words", tag=tag + "w", align_bytes=64)
+            scales = pool.tile([P, width], U8, name="scales", tag=tag + "s", align_bytes=64)
+            return words, scales
+
+        def quantise_into(coded_pair, a, b, values):
+            nc.vector.quantize_mx(out=coded_pair[0][:, a:b].bitcast(FP8X4), scales=coded_pair[1][:, a:b], in_=values)
+
+        def quantise(values, width, tag, pool):
+            coded_pair = new_codes(width, tag, pool)
+            quantise_into(coded_pair, 0, width, values)
+            return coded_pair
+
+        def quantise_piece(piece, values):
+            kind, e, o, c0, c1 = piece
+            if kind == "w2":
+                second[e] = quantise(values, c1 - c0, "second", tail)
+            else:
+                codes[piece] = quantise(values, c1 - c0, "first", coded)
+
+        def ranges(kind, e):
+            return LAST_RANGES if kind == "w3" and e == E - 1 else ((0, H),)
+
+        def pair_order(ap):
+            return ap.rearrange("s (p u b) -> s u p b", u=2, b=2)
+
+        def multiply(piece):
+            kind, e, o, c0, c1 = piece
+            if kind == "w2":
+                return
+            words, scales = codes[piece]
+            slots = slice(e * C, (e + 1) * C)
+            for a, b in ranges(kind, e):
+                if a < c0 or b > c1:
+                    continue
+                if o == 0:
+                    banks[kind, e, a] = sums.tile([C, b - a], F32, name="bank", tag="bank")
+                nc.tensor.matmul_mx(
+                    out=banks[kind, e, a][:], lhsT=slot_words[o][:, slots].bitcast(FP8X4), lhsT_scale=slot_scales[4 * o:P, slots],
+                    rhs=words[:, a - c0:b - c0].bitcast(FP8X4), rhs_scale=scales[:, a - c0:b - c0],
+                    start=(o == 0), stop=(o == PASSES - 1))
+
+        def sigmoid(e):
+            sigs[e] = tail.tile([C, 2, P, 2], F32, name="sig", tag="sig")
+            nc.scalar.activation(sigs[e][:], pair_order(banks["w1", e, 0][:]), SIGMOID)
+
+        def gated(e, a=0, b=H):
+            if e not in hidden:
+                hidden[e] = tail.tile([C, 2, P, 2], BF16, name="hidden", tag="hidden")
+            ps = slice(a // PACK, b // PACK)
+            nc.vector.tensor_tensor(hidden[e][:, :, ps, :], sigs[e][:, :, ps, :], pair_order(banks["w3", e, a][:]), MULT)
+
+        grouped, hidden_codes, y_banks, ys = {}, {}, {}, {}
+
+        def turn_hidden(e):
+            turned = small.tile([P, 2, C], F32, name="turned", tag="turned")
+            pairs = hidden[e][:].rearrange("s u p b -> s (u p b)").bitcast(F32)
+            for u in range(2):
+                nc.tensor.transpose(turned[:, u, :], pairs[:, u * P:(u + 1) * P], ident[:])
+            grouped[e] = tail.tile([P, C * PACK], BF16, name="grouped", tag="grouped", align_bytes=64)
+            nc.scalar.copy(grouped[e][:].bitcast(F32).rearrange("p (s u) -> p s u", u=2), turned[:].rearrange("p u s -> p s u"))
+
+        def second_layer(e):
+            words, scales = quantise(grouped[e][:], C, "hidden", tail)
+            y_bank = y_banks[e] = small.tile([N, C], F32, name="y_bank", tag="y_bank")
+            nc.tensor.matmul_mx(out=y_bank[:], lhsT=second[e][0][:].bitcast(FP8X4), lhsT_scale=second[e][1][:],
+                                rhs=words[:].bitcast(FP8X4), rhs_scale=scales[:], start=True, stop=True)
+
+        def scatter(e):
+            ys[e] = tail.tile([N, C], F32, name="y", tag="y")
+            nc.scalar.copy(ys[e][:], y_banks[e][:])
+            nc.vector.tensor_tensor(result[:].indirect(offsets[:, e * LIST_COLS:(e + 1) * LIST_COLS]),
+                                    ys[e][:], gate_wide[:, e * C:(e + 1) * C], MULT)
+
+        count = len(pieces)
+        nc.sync.dma_start(offsets[:], offs)
+        for o in range(PASSES):
+            load_words(o)
+        load_scales()
+        load(pieces[0])
+        load(pieces[1])
+        nc.sync.dma_start(gate_rows[:], gate[0].rearrange("(p f) -> p f", f=PACK))
+        for i in range(2, LOAD_AHEAD):
+            load(pieces[i])
+        for o in range(PASSES):
+            gather_words(o)
+        nc.vector.tensor_copy(slot_scales[:], token_scales[:].indirect(offsets[:]))
+        stages = {}
+        for i, (kind, e, o, c0, c1) in enumerate(pieces):
+            if kind == "w1" and o == PASSES - 1:
+                stages.setdefault(i + 1, []).append((sigmoid, e))
+            if kind == "w3" and o == PASSES - 1 and e < E - 1:
+                for delay, stage in enumerate((gated, turn_hidden, second_layer, scatter)):
+                    stages.setdefault(i + 1 + delay, []).append((stage, e))
+        steady = count - 5
+        for i in range(steady):
+            if i + LOAD_AHEAD < count:
+                load(pieces[i + LOAD_AHEAD])
+            values = interleave(i, stages.get(i, []))
+            if i == 4:
+                spread_gate()
+            quantise_piece(pieces[i], values)
+            multiply(pieces[i])
+
+        whole, wide, middle, final, last_w2 = pieces[steady:]
+        last = E - 1
+        half = H // 2
+        low = round_columns(nc.scalar.copy, 512, whole, 0, half)
+        high = round_columns(nc.vector.tensor_copy, 256, whole, half, H)
+        codes[whole] = new_codes(H, "first", coded)
+        quantise_into(codes[whole], half, H, high)
+        quantise_into(codes[whole], 0, half, low)
+        multiply(whole)
+        wide_part = round_columns(nc.scalar.copy, 0, wide, 0, 256)
+        middle_part = round_columns(nc.vector.tensor_copy, 512, middle, 0, 128)
+        final_part = round_columns(nc.scalar.copy, 256, final, 0, 128)
+        quantise_piece(middle, middle_part)
+        multiply(middle)
+        quantise_piece(wide, wide_part)
+        multiply(wide)
+        gated(last, 256, 384)
+        gated(last, 0, 256)
+        quantise_piece(final, final_part)
+        multiply(final)
+        w2_part = round_columns(nc.scalar.copy, 0, last_w2, 0, N)
+        gated(last, 384, 512)
+        quantise_piece(last_w2, w2_part)
+        turn_hidden(last)
+        second_layer(last)
+        scatter(last)
+        nc.sync.dma_start(out, result[:])

@@ -24,8 +24,6 @@ K_PASS = P * PACK
 PASSES = K // K_PASS
 LIST_COLS = C // 16
 SCALAR_EIGHTHS = 5
-SCALAR_COLS = H * SCALAR_EIGHTHS // 8
-LAST_RANGES = ((0, 256), (256, 384), (384, 512))
 LOAD_AHEAD = 10
 
 
@@ -34,6 +32,7 @@ def tile_moe_pkd_glu_sigmoid_kernel(tc, x_words, x_scales, w1, w3, w2, gate, off
     with ExitStack() as ctx:
         keep = ctx.enter_context(tc.tile_pool(name="keep", bufs=1))
         raw_pool = ctx.enter_context(tc.tile_pool(name="raw", bufs=LOAD_AHEAD + 2))
+        work = ctx.enter_context(tc.tile_pool(name="work", bufs=4))
         coded = ctx.enter_context(tc.tile_pool(name="coded", bufs=4))
         tail = ctx.enter_context(tc.tile_pool(name="tail", bufs=2))
         sums = ctx.enter_context(tc.psum_pool(name="sums", bufs=6))
@@ -47,7 +46,6 @@ def tile_moe_pkd_glu_sigmoid_kernel(tc, x_words, x_scales, w1, w3, w2, gate, off
         gate_rows = keep.tile([P, PACK], F32, name="gate_rows")
         gate_wide = keep.tile([P, S], F32, name="gate_wide")
         ident = keep.tile([P, P], F32, name="ident")
-        staging = keep.tile([P, (H + SCALAR_COLS) * PACK], BF16, name="staging", align_bytes=64)
         result = keep.tile([N, T], F32, name="result")
 
         nc.gpsimd.memset(token_scales[:].bitcast(I32), 0)
@@ -73,18 +71,14 @@ def tile_moe_pkd_glu_sigmoid_kernel(tc, x_words, x_scales, w1, w3, w2, gate, off
 
         pieces = []
         for e in range(E):
-            last = e == E - 1
-            for o in range(PASSES):
-                pieces.append(("w1", e, o, 0, H))
-            if not last:
-                pieces.append(("w2", e, 0, 0, N))
-            for o in range(PASSES):
-                if last and o == PASSES - 1:
-                    pieces.extend(("w3", e, o, c0, c1) for c0, c1 in LAST_RANGES)
-                else:
-                    pieces.append(("w3", e, o, 0, H))
-            if last:
-                pieces.append(("w2", e, 0, 0, N))
+            pieces.extend(("w1", e, o, 0, H) for o in range(PASSES))
+            pieces.append(("w3", e, 0, 0, H))
+            pieces.append(("w2", e, 0, 0, N))
+            pieces.append(("w3", e, 1, 0, H))
+            if e < E - 1:
+                pieces.append(("w3", e, 2, 0, H))
+            else:
+                pieces.extend([("w3", e, 2, 0, H // 2), ("w3", e, 2, H // 2, H)])
         source = {"w1": w1, "w3": w3, "w2": w2}
         raw, rounded, codes, banks, sigs, hidden, second = {}, {}, {}, {}, {}, {}, {}
 
@@ -94,30 +88,33 @@ def tile_moe_pkd_glu_sigmoid_kernel(tc, x_words, x_scales, w1, w3, w2, gate, off
             rows = source[kind][e, o * K_PASS:(o + 1) * K_PASS, c0:c1]
             nc.sync.dma_start(raw[piece][:], rows.rearrange("(p j) c -> p j c", j=PACK))
 
-        def round_columns(copy, at, piece, a, b):
-            target = staging[:, at * PACK:(at + b - a) * PACK]
-            copy(target.rearrange("p (c i j) -> p c j i", i=4, j=PACK),
+        def round_columns(copy, target, piece, a, b):
+            copy(target.rearrange("p (c i) j -> p c j i", i=4),
                  raw[piece][:, :, a:b].rearrange("p j (c i) -> p c j i", i=4))
-            return target
 
-        def interleave(i, between):
-            piece = pieces[i]
+        def scalar_columns(piece):
+            kind, e, o, c0, c1 = piece
+            if kind == "w2" or (kind == "w1" and o < 2 and e > 0):
+                return c1 - c0
+            if kind == "w3" and o == 0:
+                return 0
+            return (c1 - c0) * SCALAR_EIGHTHS // 8
+
+        def interleave(piece, between):
             width = piece[4] - piece[3]
-            by_scalar = width * SCALAR_EIGHTHS // 8
-            by_vector = width - by_scalar
-            if i % 2 == 0:
-                start = SCALAR_COLS - by_scalar
-                round_columns(nc.scalar.copy, start, piece, 0, by_scalar)
-            else:
-                start = H - by_vector
-                round_columns(nc.scalar.copy, H, piece, by_vector, width)
+            rounded[piece] = work.tile([P, width, PACK], BF16, name="rounded", tag="rounded", align_bytes=64)
+            cut = scalar_columns(piece)
+            if cut > 0:
+                round_columns(nc.scalar.copy, rounded[piece][:, 0:cut, :], piece, 0, cut)
             for stage, e in between:
                 stage(e)
-            if i % 2 == 0:
-                round_columns(nc.vector.tensor_copy, SCALAR_COLS, piece, by_scalar, width)
-            else:
-                round_columns(nc.vector.tensor_copy, start, piece, 0, by_vector)
-            return staging[:, start * PACK:(start + width) * PACK]
+            if cut < width:
+                round_columns(nc.vector.tensor_copy, rounded[piece][:, cut:width, :], piece, cut, width)
+
+        def interleave_part(copy, piece, a, b):
+            part = work.tile([P, b - a, PACK], BF16, name="part", tag="rounded", align_bytes=64)
+            round_columns(copy, part[:], piece, a, b)
+            return part
 
         def new_codes(width, tag, pool):
             words = pool.tile([P, width], U32, name="words", tag=tag + "w", align_bytes=64)
@@ -132,15 +129,15 @@ def tile_moe_pkd_glu_sigmoid_kernel(tc, x_words, x_scales, w1, w3, w2, gate, off
             quantise_into(coded_pair, 0, width, values)
             return coded_pair
 
+        def flat(tile):
+            return tile[:].rearrange("p c j -> p (c j)")
+
         def quantise_piece(piece, values):
             kind, e, o, c0, c1 = piece
             if kind == "w2":
                 second[e] = quantise(values, c1 - c0, "second", tail)
             else:
                 codes[piece] = quantise(values, c1 - c0, "first", coded)
-
-        def ranges(kind, e):
-            return LAST_RANGES if kind == "w3" and e == E - 1 else ((0, H),)
 
         def pair_order(ap):
             return ap.rearrange("s (p u b) -> s u p b", u=2, b=2)
@@ -151,35 +148,30 @@ def tile_moe_pkd_glu_sigmoid_kernel(tc, x_words, x_scales, w1, w3, w2, gate, off
                 return
             words, scales = codes[piece]
             slots = slice(e * C, (e + 1) * C)
-            for a, b in ranges(kind, e):
-                if a < c0 or b > c1:
-                    continue
-                if o == 0:
-                    banks[kind, e, a] = sums.tile([C, b - a], F32, name="bank", tag="bank")
-                nc.tensor.matmul_mx(
-                    out=banks[kind, e, a][:], lhsT=slot_words[o][:, slots].bitcast(FP8X4), lhsT_scale=slot_scales[4 * o:P, slots],
-                    rhs=words[:, a - c0:b - c0].bitcast(FP8X4), rhs_scale=scales[:, a - c0:b - c0],
-                    start=(o == 0), stop=(o == PASSES - 1))
+            if o == 0:
+                banks[kind, e] = sums.tile([C, H], F32, name="bank", tag="bank")
+            nc.tensor.matmul_mx(
+                out=banks[kind, e][:], lhsT=slot_words[o][:, slots].bitcast(FP8X4), lhsT_scale=slot_scales[4 * o:P, slots],
+                rhs=words[:].bitcast(FP8X4), rhs_scale=scales[:], start=(o == 0), stop=(o == PASSES - 1))
 
         def sigmoid(e):
             sigs[e] = tail.tile([C, 2, P, 2], F32, name="sig", tag="sig")
-            nc.scalar.activation(sigs[e][:], pair_order(banks["w1", e, 0][:]), SIGMOID)
+            nc.scalar.activation(sigs[e][:], pair_order(banks["w1", e][:]), SIGMOID)
 
-        def gated(e, a=0, b=H):
-            if e not in hidden:
-                hidden[e] = tail.tile([C, 2, P, 2], BF16, name="hidden", tag="hidden")
-            ps = slice(a // PACK, b // PACK)
-            nc.vector.tensor_tensor(hidden[e][:, :, ps, :], sigs[e][:, :, ps, :], pair_order(banks["w3", e, a][:]), MULT)
+        def gated(e):
+            hidden[e] = tail.tile([C, 2, P, 2], BF16, name="hidden", tag="hidden")
+            nc.vector.tensor_tensor(hidden[e][:], sigs[e][:], pair_order(banks["w3", e][:]), MULT)
 
         grouped, hidden_codes, y_banks, ys = {}, {}, {}, {}
 
         def turn_hidden(e):
+            copy = nc.scalar.copy if e == E - 1 else nc.vector.tensor_copy
             turned = small.tile([P, 2, C], F32, name="turned", tag="turned")
             pairs = hidden[e][:].rearrange("s u p b -> s (u p b)").bitcast(F32)
             for u in range(2):
                 nc.tensor.transpose(turned[:, u, :], pairs[:, u * P:(u + 1) * P], ident[:])
             grouped[e] = tail.tile([P, C * PACK], BF16, name="grouped", tag="grouped", align_bytes=64)
-            nc.scalar.copy(grouped[e][:].bitcast(F32).rearrange("p (s u) -> p s u", u=2), turned[:].rearrange("p u s -> p s u"))
+            copy(grouped[e][:].bitcast(F32).rearrange("p (s u) -> p s u", u=2), turned[:].rearrange("p u s -> p s u"))
 
         def second_layer(e):
             words, scales = quantise(grouped[e][:], C, "hidden", tail)
@@ -188,10 +180,14 @@ def tile_moe_pkd_glu_sigmoid_kernel(tc, x_words, x_scales, w1, w3, w2, gate, off
                                 rhs=words[:].bitcast(FP8X4), rhs_scale=scales[:], start=True, stop=True)
 
         def scatter(e):
-            ys[e] = tail.tile([N, C], F32, name="y", tag="y")
-            nc.scalar.copy(ys[e][:], y_banks[e][:])
+            if e < E - 1:
+                y = sigs[e + 1][:].rearrange("s u p b -> s (u p b)")[:, 0:C]
+                nc.vector.tensor_copy(y, y_banks[e][:])
+            else:
+                y = tail.tile([N, C], F32, name="y")[:]
+                nc.scalar.copy(y, y_banks[e][:])
             nc.vector.tensor_tensor(result[:].indirect(offsets[:, e * LIST_COLS:(e + 1) * LIST_COLS]),
-                                    ys[e][:], gate_wide[:, e * C:(e + 1) * C], MULT)
+                                    y, gate_wide[:, e * C:(e + 1) * C], MULT)
 
         count = len(pieces)
         nc.sync.dma_start(offsets[:], offs)
@@ -211,41 +207,39 @@ def tile_moe_pkd_glu_sigmoid_kernel(tc, x_words, x_scales, w1, w3, w2, gate, off
             if kind == "w1" and o == PASSES - 1:
                 stages.setdefault(i + 1, []).append((sigmoid, e))
             if kind == "w3" and o == PASSES - 1 and e < E - 1:
-                for delay, stage in enumerate((gated, turn_hidden, second_layer, scatter)):
+                for delay, stage in enumerate((gated, turn_hidden, second_layer)):
                     stages.setdefault(i + 1 + delay, []).append((stage, e))
-        steady = count - 5
+                if e > 0:
+                    stages[i + 1].append((scatter, e - 1))
+        steady = count - 3
         for i in range(steady):
             if i + LOAD_AHEAD < count:
                 load(pieces[i + LOAD_AHEAD])
-            values = interleave(i, stages.get(i, []))
+            interleave(pieces[i], stages.get(i, []))
             if i == 4:
                 spread_gate()
-            quantise_piece(pieces[i], values)
+            quantise_piece(pieces[i], flat(rounded[pieces[i]]))
             multiply(pieces[i])
 
-        whole, wide, middle, final, last_w2 = pieces[steady:]
+        whole, first_half, second_half = pieces[steady:]
         last = E - 1
         half = H // 2
-        low = round_columns(nc.scalar.copy, 512, whole, 0, half)
-        high = round_columns(nc.vector.tensor_copy, 256, whole, half, H)
+        quarter = half * SCALAR_EIGHTHS // 8
+        low = interleave_part(nc.scalar.copy, whole, 0, half)
+        high = interleave_part(nc.vector.tensor_copy, whole, half, H)
         codes[whole] = new_codes(H, "first", coded)
-        quantise_into(codes[whole], half, H, high)
-        quantise_into(codes[whole], 0, half, low)
+        quantise_into(codes[whole], half, H, flat(high))
+        quantise_into(codes[whole], 0, half, flat(low))
         multiply(whole)
-        wide_part = round_columns(nc.scalar.copy, 0, wide, 0, 256)
-        middle_part = round_columns(nc.vector.tensor_copy, 512, middle, 0, 128)
-        final_part = round_columns(nc.scalar.copy, 256, final, 0, 128)
-        quantise_piece(middle, middle_part)
-        multiply(middle)
-        quantise_piece(wide, wide_part)
-        multiply(wide)
-        gated(last, 256, 384)
-        gated(last, 0, 256)
-        quantise_piece(final, final_part)
-        multiply(final)
-        w2_part = round_columns(nc.scalar.copy, 0, last_w2, 0, N)
-        gated(last, 384, 512)
-        quantise_piece(last_w2, w2_part)
+        codes[second_half] = new_codes(H, "first", coded)
+        for piece in (first_half, second_half):
+            part = work.tile([P, half, PACK], BF16, name="part", tag="rounded", align_bytes=64)
+            round_columns(nc.scalar.copy, part[:, 0:quarter, :], piece, 0, quarter)
+            round_columns(nc.vector.tensor_copy, part[:, quarter:half, :], piece, quarter, half)
+            quantise_into(codes[second_half], piece[3], piece[4], flat(part))
+        multiply(second_half)
+        gated(last)
+        scatter(last - 1)
         turn_hidden(last)
         second_layer(last)
         scatter(last)

@@ -22,13 +22,17 @@ P = 128
 PACK = 4
 K_PASS = P * PACK
 PASSES = K // K_PASS
+HALF = H // 2
 LIST_COLS = C // 16
+RUN = 4
 SCALAR_EIGHTHS = 5
+SCALAR_EIGHTHS_BUSY_VECTOR = 6
 LOAD_AHEAD = 10
 
 
 def tile_moe_pkd_glu_sigmoid_kernel(tc, x_words, x_scales, w1, w3, w2, gate, offs, out):
     nc = tc.nc
+    last = E - 1
     with ExitStack() as ctx:
         keep = ctx.enter_context(tc.tile_pool(name="keep", bufs=1))
         raw_pool = ctx.enter_context(tc.tile_pool(name="raw", bufs=LOAD_AHEAD + 2))
@@ -39,12 +43,15 @@ def tile_moe_pkd_glu_sigmoid_kernel(tc, x_words, x_scales, w1, w3, w2, gate, off
         small = ctx.enter_context(tc.psum_pool(name="small", bufs=1))
 
         offsets = keep.tile([P, S // 16], U16, name="offsets")
-        token_words = [keep.tile([P, T], I32, name="token_words%d" % o) for o in range(PASSES)]
+        token_words = keep.tile([P, PASSES, T], I32, name="token_words")
         token_scales = keep.tile([P, T], U8, name="token_scales")
-        slot_words = [keep.tile([P, S], U32, name="slot_words%d" % o, align_bytes=64) for o in range(PASSES)]
+        slot_words = keep.tile([P, PASSES, S], U32, name="slot_words", align_bytes=64)
         slot_scales = keep.tile([P, S], U8, name="slot_scales", align_bytes=64)
+        w2_raw = keep.tile([P, E, PACK, N], F32, name="w2_raw")
+        w2_words = keep.tile([P, E * N], U32, name="w2_words", align_bytes=64)
+        w2_scales = keep.tile([P, E * N], U8, name="w2_scales", align_bytes=64)
         gate_rows = keep.tile([P, PACK], F32, name="gate_rows")
-        gate_wide = keep.tile([P, S], F32, name="gate_wide")
+        gate_wide = keep.tile([N, S], F32, name="gate_wide")
         ident = keep.tile([P, P], F32, name="ident")
         result = keep.tile([N, T], F32, name="result")
 
@@ -52,35 +59,10 @@ def tile_moe_pkd_glu_sigmoid_kernel(tc, x_words, x_scales, w1, w3, w2, gate, off
         nc.gpsimd.memset(result[:], 0.0)
         make_identity(nc, ident[:])
 
-        def load_words(o):
-            nc.sync.dma_start(token_words[o][:], x_words[o].rearrange("p t r -> p (t r)").bitcast(I32))
-
-        def load_scales():
-            for q in range(4):
-                nc.sync.dma_start(token_scales[32 * q:32 * q + 4 * PASSES, :].bitcast(I32),
-                                  x_scales[:, 4 * q:4 * q + 4, :].bitcast(I32))
-
-        def gather_words(o):
-            nc.vector.tensor_copy(slot_words[o][:], token_words[o][:].bitcast(U32).indirect(offsets[:]))
-
-        def spread_gate():
-            turned = small.tile([P, PACK, P], F32, name="turned", tag="turned")
-            for f in range(PACK):
-                nc.tensor.transpose(turned[:, f, :], gate_rows[:, f:f + 1].to_broadcast([P, P]), ident[:])
-            nc.scalar.copy(gate_wide[:].rearrange("n (p f) -> n p f", f=PACK), turned[:].rearrange("n f p -> n p f"))
-
-        pieces = []
-        for e in range(E):
-            pieces.extend(("w1", e, o, 0, H) for o in range(PASSES))
-            pieces.append(("w3", e, 0, 0, H))
-            pieces.append(("w2", e, 0, 0, N))
-            pieces.append(("w3", e, 1, 0, H))
-            if e < E - 1:
-                pieces.append(("w3", e, 2, 0, H))
-            else:
-                pieces.extend([("w3", e, 2, 0, H // 2), ("w3", e, 2, H // 2, H)])
-        source = {"w1": w1, "w3": w3, "w2": w2}
-        raw, rounded, codes, banks, sigs, hidden, second = {}, {}, {}, {}, {}, {}, {}
+        pieces = [(kind, e, o, 0, H) for e in range(E) for kind in ("w1", "w3") for o in range(PASSES)]
+        pieces[-1:] = [("w3", last, PASSES - 1, 0, HALF), ("w3", last, PASSES - 1, HALF, H)]
+        source = {"w1": w1, "w3": w3}
+        raw, banks, sigs, hidden, grouped, y_banks = {}, {}, {}, {}, {}, {}
 
         def load(piece):
             kind, e, o, c0, c1 = piece
@@ -88,157 +70,142 @@ def tile_moe_pkd_glu_sigmoid_kernel(tc, x_words, x_scales, w1, w3, w2, gate, off
             rows = source[kind][e, o * K_PASS:(o + 1) * K_PASS, c0:c1]
             nc.sync.dma_start(raw[piece][:], rows.rearrange("(p j) c -> p j c", j=PACK))
 
-        def round_columns(copy, target, piece, a, b):
-            copy(target.rearrange("p (c i) j -> p c j i", i=4),
-                 raw[piece][:, :, a:b].rearrange("p j (c i) -> p c j i", i=4))
+        def round_columns(copy, target, rows):
+            copy(target.rearrange("p (c i) j -> p c j i", i=RUN), rows.rearrange("p j (c i) -> p c j i", i=RUN))
+
+        def round_shared(rows, width, cut):
+            rounded = work.tile([P, width, PACK], BF16, name="rounded", tag="rounded", align_bytes=64)
+            if cut > 0:
+                round_columns(nc.scalar.copy, rounded[:, 0:cut, :], rows[:, :, 0:cut])
+            if cut < width:
+                round_columns(nc.vector.tensor_copy, rounded[:, cut:width, :], rows[:, :, cut:width])
+            return rounded[:].rearrange("p c j -> p (c j)")
 
         def scalar_columns(piece):
             kind, e, o, c0, c1 = piece
-            if kind == "w2" or (kind == "w1" and o < 2 and e > 0):
-                return c1 - c0
+            if kind == "w1" and o < 2 and e > 0:
+                return H * SCALAR_EIGHTHS_BUSY_VECTOR // 8
             if kind == "w3" and o == 0:
                 return 0
             return (c1 - c0) * SCALAR_EIGHTHS // 8
 
-        def interleave(piece, between):
-            width = piece[4] - piece[3]
-            rounded[piece] = work.tile([P, width, PACK], BF16, name="rounded", tag="rounded", align_bytes=64)
-            cut = scalar_columns(piece)
-            if cut > 0:
-                round_columns(nc.scalar.copy, rounded[piece][:, 0:cut, :], piece, 0, cut)
-            for stage, e in between:
-                stage(e)
-            if cut < width:
-                round_columns(nc.vector.tensor_copy, rounded[piece][:, cut:width, :], piece, cut, width)
+        def new_codes(pool, width, tag):
+            words = pool.tile([P, width], U32, name="words", tag=tag + "_words", align_bytes=64)
+            scales = pool.tile([P, width], U8, name="scales", tag=tag + "_scales", align_bytes=64)
+            return words[:], scales[:]
 
-        def interleave_part(copy, piece, a, b):
-            part = work.tile([P, b - a, PACK], BF16, name="part", tag="rounded", align_bytes=64)
-            round_columns(copy, part[:], piece, a, b)
-            return part
+        def quantise(words, scales, values):
+            nc.vector.quantize_mx(out=words.bitcast(FP8X4), scales=scales, in_=values)
 
-        def new_codes(width, tag, pool):
-            words = pool.tile([P, width], U32, name="words", tag=tag + "w", align_bytes=64)
-            scales = pool.tile([P, width], U8, name="scales", tag=tag + "s", align_bytes=64)
-            return words, scales
-
-        def quantise_into(coded_pair, a, b, values):
-            nc.vector.quantize_mx(out=coded_pair[0][:, a:b].bitcast(FP8X4), scales=coded_pair[1][:, a:b], in_=values)
-
-        def quantise(values, width, tag, pool):
-            coded_pair = new_codes(width, tag, pool)
-            quantise_into(coded_pair, 0, width, values)
-            return coded_pair
-
-        def flat(tile):
-            return tile[:].rearrange("p c j -> p (c j)")
-
-        def quantise_piece(piece, values):
-            kind, e, o, c0, c1 = piece
-            if kind == "w2":
-                second[e] = quantise(values, c1 - c0, "second", tail)
-            else:
-                codes[piece] = quantise(values, c1 - c0, "first", coded)
-
-        def pair_order(ap):
-            return ap.rearrange("s (p u b) -> s u p b", u=2, b=2)
-
-        def multiply(piece):
-            kind, e, o, c0, c1 = piece
-            if kind == "w2":
-                return
-            words, scales = codes[piece]
+        def multiply(kind, e, o, c0, c1, words, scales):
             slots = slice(e * C, (e + 1) * C)
             if o == 0:
-                banks[kind, e] = sums.tile([C, H], F32, name="bank", tag="bank")
+                banks[kind, e, c0] = sums.tile([C, c1 - c0], F32, name="bank", tag="bank")
             nc.tensor.matmul_mx(
-                out=banks[kind, e][:], lhsT=slot_words[o][:, slots].bitcast(FP8X4), lhsT_scale=slot_scales[4 * o:P, slots],
-                rhs=words[:].bitcast(FP8X4), rhs_scale=scales[:], start=(o == 0), stop=(o == PASSES - 1))
+                out=banks[kind, e, c0][:], lhsT=slot_words[:, o, slots].bitcast(FP8X4), lhsT_scale=slot_scales[4 * o:P, slots],
+                rhs=words.bitcast(FP8X4), rhs_scale=scales, start=(o == 0), stop=(o == PASSES - 1))
+
+        def pair_order(bank):
+            return bank[:].rearrange("s (p u b) -> s u p b", u=2, b=2)
 
         def sigmoid(e):
             sigs[e] = tail.tile([C, 2, P, 2], F32, name="sig", tag="sig")
-            nc.scalar.activation(sigs[e][:], pair_order(banks["w1", e][:]), SIGMOID)
+            nc.scalar.activation(sigs[e][:], pair_order(banks["w1", e, 0]), SIGMOID)
 
-        def gated(e):
-            hidden[e] = tail.tile([C, 2, P, 2], BF16, name="hidden", tag="hidden")
-            nc.vector.tensor_tensor(hidden[e][:], sigs[e][:], pair_order(banks["w3", e][:]), MULT)
+        def gated(e, c0, c1):
+            ps = slice(c0 // PACK, c1 // PACK)
+            target = hidden[e].rearrange("s (u p b) -> s u p b", u=2, b=2)
+            nc.vector.tensor_tensor(target[:, :, ps, :], sigs[e][:, :, ps, :], pair_order(banks["w3", e, c0]), MULT)
 
-        grouped, hidden_codes, y_banks, ys = {}, {}, {}, {}
+        def copy_out_of_bank(e):
+            return nc.scalar.copy if e == last else nc.vector.tensor_copy
 
         def turn_hidden(e):
-            copy = nc.scalar.copy if e == E - 1 else nc.vector.tensor_copy
             turned = small.tile([P, 2, C], F32, name="turned", tag="turned")
-            pairs = hidden[e][:].rearrange("s u p b -> s (u p b)").bitcast(F32)
+            pairs = hidden[e].bitcast(F32)
             for u in range(2):
                 nc.tensor.transpose(turned[:, u, :], pairs[:, u * P:(u + 1) * P], ident[:])
             grouped[e] = tail.tile([P, C * PACK], BF16, name="grouped", tag="grouped", align_bytes=64)
-            copy(grouped[e][:].bitcast(F32).rearrange("p (s u) -> p s u", u=2), turned[:].rearrange("p u s -> p s u"))
+            copy_out_of_bank(e)(grouped[e][:].bitcast(F32).rearrange("p (s u) -> p s u", u=2),
+                                turned[:].rearrange("p u s -> p s u"))
 
         def second_layer(e):
-            words, scales = quantise(grouped[e][:], C, "hidden", tail)
-            y_bank = y_banks[e] = small.tile([N, C], F32, name="y_bank", tag="y_bank")
-            nc.tensor.matmul_mx(out=y_bank[:], lhsT=second[e][0][:].bitcast(FP8X4), lhsT_scale=second[e][1][:],
-                                rhs=words[:].bitcast(FP8X4), rhs_scale=scales[:], start=True, stop=True)
+            words, scales = new_codes(tail, C, "hidden")
+            quantise(words, scales, grouped[e][:])
+            y_banks[e] = small.tile([N, C], F32, name="y_bank", tag="y_bank")
+            columns = slice(e * N, (e + 1) * N)
+            nc.tensor.matmul_mx(out=y_banks[e][:], lhsT=w2_words[:, columns].bitcast(FP8X4), lhsT_scale=w2_scales[:, columns],
+                                rhs=words.bitcast(FP8X4), rhs_scale=scales, start=True, stop=True)
 
         def scatter(e):
-            if e < E - 1:
-                y = sigs[e + 1][:].rearrange("s u p b -> s (u p b)")[:, 0:C]
-                nc.vector.tensor_copy(y, y_banks[e][:])
-            else:
-                y = tail.tile([N, C], F32, name="y")[:]
-                nc.scalar.copy(y, y_banks[e][:])
+            y = sigs[min(e + 1, last)][:].rearrange("s u p b -> s (u p b)")[:, ((e + 1) % 2) * C:((e + 1) % 2 + 1) * C]
+            copy_out_of_bank(e)(y, y_banks[e][:])
             nc.vector.tensor_tensor(result[:].indirect(offsets[:, e * LIST_COLS:(e + 1) * LIST_COLS]),
                                     y, gate_wide[:, e * C:(e + 1) * C], MULT)
 
-        count = len(pieces)
         nc.sync.dma_start(offsets[:], offs)
-        for o in range(PASSES):
-            load_words(o)
-        load_scales()
+        nc.sync.dma_start(token_words[:], x_words.rearrange("o p t r -> p o (t r)").bitcast(I32))
         load(pieces[0])
+        for q in range(4):
+            nc.sync.dma_start(token_scales[32 * q:32 * q + 4 * PASSES, :].bitcast(I32),
+                              x_scales[:, 4 * q:4 * q + 4, :].bitcast(I32))
         load(pieces[1])
         nc.sync.dma_start(gate_rows[:], gate[0].rearrange("(p f) -> p f", f=PACK))
-        for i in range(2, LOAD_AHEAD):
-            load(pieces[i])
+        nc.sync.dma_start(w2_raw[:], w2.rearrange("e (p j) n -> p e j n", j=PACK))
+        for piece in pieces[2:LOAD_AHEAD]:
+            load(piece)
+
         for o in range(PASSES):
-            gather_words(o)
+            nc.vector.tensor_copy(slot_words[:, o, :], token_words[:, o, :].bitcast(U32).indirect(offsets[:]))
         nc.vector.tensor_copy(slot_scales[:], token_scales[:].indirect(offsets[:]))
-        stages = {}
-        for i, (kind, e, o, c0, c1) in enumerate(pieces):
-            if kind == "w1" and o == PASSES - 1:
-                stages.setdefault(i + 1, []).append((sigmoid, e))
-            if kind == "w3" and o == PASSES - 1 and e < E - 1:
-                for delay, stage in enumerate((gated, turn_hidden, second_layer)):
-                    stages.setdefault(i + 1 + delay, []).append((stage, e))
-                if e > 0:
-                    stages[i + 1].append((scatter, e - 1))
-        steady = count - 3
-        for i in range(steady):
-            if i + LOAD_AHEAD < count:
+
+        gate_bank = small.tile([P, PACK, P], F32, name="gate_bank", tag="turned")
+        for f in range(PACK):
+            nc.tensor.transpose(gate_bank[:, f, :], gate_rows[:, f:f + 1].to_broadcast([P, P]), ident[:])
+        nc.scalar.copy(gate_wide[:].rearrange("n (p f) -> n p f", f=PACK), gate_bank[:].rearrange("n f p -> n p f"))
+
+        w2_rounded = work.tile([P, E * N, PACK], BF16, name="w2_rounded", tag="rounded", align_bytes=64)
+        for e in range(E):
+            round_columns(nc.scalar.copy, w2_rounded[:, e * N:(e + 1) * N, :], w2_raw[:, e, :, :])
+        quantise(w2_words[:], w2_scales[:], w2_rounded[:].rearrange("p c j -> p (c j)"))
+
+        steady = len(pieces) - 3
+        for i, piece in enumerate(pieces[:steady]):
+            kind, e, o, c0, c1 = piece
+            if i + LOAD_AHEAD < len(pieces):
                 load(pieces[i + LOAD_AHEAD])
-            interleave(pieces[i], stages.get(i, []))
-            if i == 4:
-                spread_gate()
-            quantise_piece(pieces[i], flat(rounded[pieces[i]]))
-            multiply(pieces[i])
+            values = round_shared(raw[piece], H, scalar_columns(piece))
+            if kind == "w3" and o == 0:
+                sigmoid(e)
+            if kind == "w1" and e > 0:
+                if o == 0:
+                    hidden[e - 1] = tail.tile([C, H], BF16, name="hidden", tag="hidden")[:]
+                    gated(e - 1, 0, H)
+                    if e > 1:
+                        scatter(e - 2)
+                    turn_hidden(e - 1)
+                if o == 1:
+                    second_layer(e - 1)
+            words, scales = new_codes(coded, H, "first")
+            quantise(words, scales, values)
+            for a, b in ((0, HALF), (HALF, H)) if (kind, e) == ("w3", last) else ((0, H),):
+                multiply(kind, e, o, a, b, words[:, a:b], scales[:, a:b])
 
         whole, first_half, second_half = pieces[steady:]
-        last = E - 1
-        half = H // 2
-        quarter = half * SCALAR_EIGHTHS // 8
-        low = interleave_part(nc.scalar.copy, whole, 0, half)
-        high = interleave_part(nc.vector.tensor_copy, whole, half, H)
-        codes[whole] = new_codes(H, "first", coded)
-        quantise_into(codes[whole], half, H, flat(high))
-        quantise_into(codes[whole], 0, half, flat(low))
-        multiply(whole)
-        codes[second_half] = new_codes(H, "first", coded)
+        low = round_shared(raw[whole][:, :, 0:HALF], HALF, HALF)
+        high = round_shared(raw[whole][:, :, HALF:H], HALF, 0)
+        for values, a, b in ((high, HALF, H), (low, 0, HALF)):
+            words, scales = new_codes(coded, HALF, "first")
+            quantise(words, scales, values)
+            multiply("w3", last, 1, a, b, words, scales)
         for piece in (first_half, second_half):
-            part = work.tile([P, half, PACK], BF16, name="part", tag="rounded", align_bytes=64)
-            round_columns(nc.scalar.copy, part[:, 0:quarter, :], piece, 0, quarter)
-            round_columns(nc.vector.tensor_copy, part[:, quarter:half, :], piece, quarter, half)
-            quantise_into(codes[second_half], piece[3], piece[4], flat(part))
-        multiply(second_half)
-        gated(last)
+            values = round_shared(raw[piece], HALF, scalar_columns(piece))
+            words, scales = new_codes(coded, HALF, "first")
+            quantise(words, scales, values)
+            multiply(*piece, words, scales)
+        hidden[last] = values[:, 0:H]
+        gated(last, 0, HALF)
+        gated(last, HALF, H)
         scatter(last - 1)
         turn_hidden(last)
         second_layer(last)

@@ -22,10 +22,12 @@ P = 128
 PACK = 4
 K_PASS = P * PACK
 PASSES = K // K_PASS
+QUADRANT = 32
+SCALE_ROWS = 4
 HALF = H // 2
 LIST_COLS = C // 16
 RUN = 4
-SCALAR_EIGHTHS = 5
+SCALAR_EIGHTHS = 4
 SCALAR_EIGHTHS_BUSY_VECTOR = 6
 LOAD_AHEAD = 10
 
@@ -83,7 +85,7 @@ def tile_moe_pkd_glu_sigmoid_kernel(tc, x_words, x_scales, w1, w3, w2, gate, off
 
         def scalar_columns(piece):
             kind, e, o, c0, c1 = piece
-            if kind == "w1" and o < 2 and e > 0:
+            if kind == "w1" and o < PASSES - 1 and e > 0:
                 return H * SCALAR_EIGHTHS_BUSY_VECTOR // 8
             if kind == "w3" and o == 0:
                 return 0
@@ -102,7 +104,8 @@ def tile_moe_pkd_glu_sigmoid_kernel(tc, x_words, x_scales, w1, w3, w2, gate, off
             if o == 0:
                 banks[kind, e, c0] = sums.tile([C, c1 - c0], F32, name="bank", tag="bank")
             nc.tensor.matmul_mx(
-                out=banks[kind, e, c0][:], lhsT=slot_words[:, o, slots].bitcast(FP8X4), lhsT_scale=slot_scales[4 * o:P, slots],
+                out=banks[kind, e, c0][:],
+                lhsT=slot_words[:, o, slots].bitcast(FP8X4), lhsT_scale=slot_scales[SCALE_ROWS * o:P, slots],
                 rhs=words.bitcast(FP8X4), rhs_scale=scales, start=(o == 0), stop=(o == PASSES - 1))
 
         def pair_order(bank):
@@ -134,11 +137,13 @@ def tile_moe_pkd_glu_sigmoid_kernel(tc, x_words, x_scales, w1, w3, w2, gate, off
             quantise(words, scales, grouped[e][:])
             y_banks[e] = small.tile([N, C], F32, name="y_bank", tag="y_bank")
             columns = slice(e * N, (e + 1) * N)
-            nc.tensor.matmul_mx(out=y_banks[e][:], lhsT=w2_words[:, columns].bitcast(FP8X4), lhsT_scale=w2_scales[:, columns],
+            nc.tensor.matmul_mx(out=y_banks[e][:],
+                                lhsT=w2_words[:, columns].bitcast(FP8X4), lhsT_scale=w2_scales[:, columns],
                                 rhs=words.bitcast(FP8X4), rhs_scale=scales, start=True, stop=True)
 
         def scatter(e):
-            y = sigs[min(e + 1, last)][:].rearrange("s u p b -> s (u p b)")[:, ((e + 1) % 2) * C:((e + 1) % 2 + 1) * C]
+            place = (e + 1) % 2
+            y = sigs[min(e + 1, last)][:].rearrange("s u p b -> s (u p b)")[:, place * C:(place + 1) * C]
             copy_out_of_bank(e)(y, y_banks[e][:])
             nc.vector.tensor_tensor(result[:].indirect(offsets[:, e * LIST_COLS:(e + 1) * LIST_COLS]),
                                     y, gate_wide[:, e * C:(e + 1) * C], MULT)
@@ -146,9 +151,9 @@ def tile_moe_pkd_glu_sigmoid_kernel(tc, x_words, x_scales, w1, w3, w2, gate, off
         nc.sync.dma_start(offsets[:], offs)
         nc.sync.dma_start(token_words[:], x_words.rearrange("o p t r -> p o (t r)").bitcast(I32))
         load(pieces[0])
-        for q in range(4):
-            nc.sync.dma_start(token_scales[32 * q:32 * q + 4 * PASSES, :].bitcast(I32),
-                              x_scales[:, 4 * q:4 * q + 4, :].bitcast(I32))
+        for q in range(P // QUADRANT):
+            nc.sync.dma_start(token_scales[QUADRANT * q:QUADRANT * q + SCALE_ROWS * PASSES, :].bitcast(I32),
+                              x_scales[:, SCALE_ROWS * q:SCALE_ROWS * (q + 1), :].bitcast(I32))
         load(pieces[1])
         nc.sync.dma_start(gate_rows[:], gate[0].rearrange("(p f) -> p f", f=PACK))
         nc.sync.dma_start(w2_raw[:], w2.rearrange("e (p j) n -> p e j n", j=PACK))
@@ -170,10 +175,10 @@ def tile_moe_pkd_glu_sigmoid_kernel(tc, x_words, x_scales, w1, w3, w2, gate, off
         quantise(w2_words[:], w2_scales[:], w2_rounded[:].rearrange("p c j -> p (c j)"))
 
         steady = len(pieces) - 3
-        for i, piece in enumerate(pieces[:steady]):
+        for index, piece in enumerate(pieces[:steady]):
             kind, e, o, c0, c1 = piece
-            if i + LOAD_AHEAD < len(pieces):
-                load(pieces[i + LOAD_AHEAD])
+            if index + LOAD_AHEAD < len(pieces):
+                load(pieces[index + LOAD_AHEAD])
             values = round_shared(raw[piece], H, scalar_columns(piece))
             if kind == "w3" and o == 0:
                 sigmoid(e)
@@ -197,7 +202,7 @@ def tile_moe_pkd_glu_sigmoid_kernel(tc, x_words, x_scales, w1, w3, w2, gate, off
         for values, a, b in ((high, HALF, H), (low, 0, HALF)):
             words, scales = new_codes(coded, HALF, "first")
             quantise(words, scales, values)
-            multiply("w3", last, 1, a, b, words, scales)
+            multiply("w3", last, PASSES - 2, a, b, words, scales)
         for piece in (first_half, second_half):
             values = round_shared(raw[piece], HALF, scalar_columns(piece))
             words, scales = new_codes(coded, HALF, "first")

from contextlib import ExitStack

import concourse.mybir as mybir
from concourse.masks import make_identity

K, T, E, C, H, N = 1536, 1024, 4, 128, 512, 128
S = E * C
FLOPS = 2 * S * (2 * K * H + H * N)
BYTES = K * T + K * T // 32 + 4 * E * (2 * K * H + H * N) + 4 * S + 2 * 128 * S // 16 + 4 * N * T

F32 = mybir.dt.float32
BF16 = mybir.dt.bfloat16
I32 = mybir.dt.int32
U32 = mybir.dt.uint32
U16 = mybir.dt.uint16
U8 = mybir.dt.uint8
FP8X4 = mybir.dt.float8_e4m3fn_x4
MULT = mybir.AluOpType.mult
SIGMOID = mybir.ActivationFunctionType.Sigmoid

P = 128
PACK = 4
K_PASS = P * PACK
PASSES = K // K_PASS
QUADRANT = 32
SCALE_ROWS = 4
HALF = H // 2
LIST_COLS = C // 16
RUN = 4
SCALAR_EIGHTHS = 4
SCALAR_EIGHTHS_BUSY_VECTOR = 6
LOAD_AHEAD = 10


def tile_moe_pkd_glu_sigmoid_kernel(tc, x_words, x_scales, w1, w3, w2, gate, offs, out):
    nc = tc.nc
    last = E - 1
    with ExitStack() as ctx:
        keep = ctx.enter_context(tc.tile_pool(name="keep", bufs=1))
        raw_pool = ctx.enter_context(tc.tile_pool(name="raw", bufs=LOAD_AHEAD + 2))
        work = ctx.enter_context(tc.tile_pool(name="work", bufs=4))
        coded = ctx.enter_context(tc.tile_pool(name="coded", bufs=4))
        tail = ctx.enter_context(tc.tile_pool(name="tail", bufs=2))
        sums = ctx.enter_context(tc.psum_pool(name="sums", bufs=6))
        small = ctx.enter_context(tc.psum_pool(name="small", bufs=1))

        offsets = keep.tile([P, S // 16], U16, name="offsets")
        token_words = keep.tile([P, PASSES, T], I32, name="token_words")
        token_scales = keep.tile([P, T], U8, name="token_scales")
        slot_words = keep.tile([P, PASSES, S], U32, name="slot_words", align_bytes=64)
        slot_scales = keep.tile([P, S], U8, name="slot_scales", align_bytes=64)
        w2_raw = keep.tile([P, E, PACK, N], F32, name="w2_raw")
        w2_words = keep.tile([P, E * N], U32, name="w2_words", align_bytes=64)
        w2_scales = keep.tile([P, E * N], U8, name="w2_scales", align_bytes=64)
        gate_rows = keep.tile([P, PACK], F32, name="gate_rows")
        gate_wide = keep.tile([N, S], F32, name="gate_wide")
        ident = keep.tile([P, P], F32, name="ident")
        result = keep.tile([N, T], F32, name="result")

        nc.gpsimd.memset(token_scales[:].bitcast(I32), 0)
        nc.gpsimd.memset(result[:], 0.0)
        make_identity(nc, ident[:])

        pieces = [(kind, e, o, 0, H) for e in range(E) for kind in ("w1", "w3") for o in range(PASSES)]
        pieces[-1:] = [("w3", last, PASSES - 1, 0, HALF), ("w3", last, PASSES - 1, HALF, H)]
        source = {"w1": w1, "w3": w3}
        raw, banks, sigs, hidden, grouped, y_banks = {}, {}, {}, {}, {}, {}

        def load(piece):
            kind, e, o, c0, c1 = piece
            raw[piece] = raw_pool.tile([P, PACK, c1 - c0], F32, name="raw", tag="raw")
            rows = source[kind][e, o * K_PASS:(o + 1) * K_PASS, c0:c1]
            nc.sync.dma_start(raw[piece][:], rows.rearrange("(p j) c -> p j c", j=PACK))

        def round_columns(copy, target, rows):
            copy(target.rearrange("p (c i) j -> p c j i", i=RUN), rows.rearrange("p j (c i) -> p c j i", i=RUN))

        def round_shared(rows, width, cut):
            rounded = work.tile([P, width, PACK], BF16, name="rounded", tag="rounded", align_bytes=64)
            if cut > 0:
                round_columns(nc.scalar.copy, rounded[:, 0:cut, :], rows[:, :, 0:cut])
            if cut < width:
                round_columns(nc.vector.tensor_copy, rounded[:, cut:width, :], rows[:, :, cut:width])
            return rounded[:].rearrange("p c j -> p (c j)")

        def scalar_columns(piece):
            kind, e, o, c0, c1 = piece
            if kind == "w1" and o < PASSES - 1 and e > 0:
                return H * SCALAR_EIGHTHS_BUSY_VECTOR // 8
            if kind == "w3" and o == 0:
                return 0
            return (c1 - c0) * SCALAR_EIGHTHS // 8

        def new_codes(pool, width, tag):
            words = pool.tile([P, width], U32, name="words", tag=tag + "_words", align_bytes=64)
            scales = pool.tile([P, width], U8, name="scales", tag=tag + "_scales", align_bytes=64)
            return words[:], scales[:]

        def quantise(words, scales, values):
            nc.vector.quantize_mx(out=words.bitcast(FP8X4), scales=scales, in_=values)

        def multiply(kind, e, o, c0, c1, words, scales):
            slots = slice(e * C, (e + 1) * C)
            if o == 0:
                banks[kind, e, c0] = sums.tile([C, c1 - c0], F32, name="bank", tag="bank")
            nc.tensor.matmul_mx(
                out=banks[kind, e, c0][:],
                lhsT=slot_words[:, o, slots].bitcast(FP8X4), lhsT_scale=slot_scales[SCALE_ROWS * o:P, slots],
                rhs=words.bitcast(FP8X4), rhs_scale=scales, start=(o == 0), stop=(o == PASSES - 1))

        def pair_order(bank):
            return bank[:].rearrange("s (p u b) -> s u p b", u=2, b=2)

        def sigmoid(e):
            sigs[e] = tail.tile([C, 2, P, 2], F32, name="sig", tag="sig")
            nc.scalar.activation(sigs[e][:], pair_order(banks["w1", e, 0]), SIGMOID)

        def gated(e, c0, c1):
            ps = slice(c0 // PACK, c1 // PACK)
            target = hidden[e].rearrange("s (u p b) -> s u p b", u=2, b=2)
            nc.vector.tensor_tensor(target[:, :, ps, :], sigs[e][:, :, ps, :], pair_order(banks["w3", e, c0]), MULT)

        def copy_out_of_bank(e):
            return nc.scalar.copy if e == last else nc.vector.tensor_copy

        def turn_hidden(e):
            turned = small.tile([P, 2, C], F32, name="turned", tag="turned")
            pairs = hidden[e].bitcast(F32)
            for u in range(2):
                nc.tensor.transpose(turned[:, u, :], pairs[:, u * P:(u + 1) * P], ident[:])
            grouped[e] = tail.tile([P, C * PACK], BF16, name="grouped", tag="grouped", align_bytes=64)
            copy_out_of_bank(e)(grouped[e][:].bitcast(F32).rearrange("p (s u) -> p s u", u=2),
                                turned[:].rearrange("p u s -> p s u"))

        def second_layer(e):
            words, scales = new_codes(tail, C, "hidden")
            quantise(words, scales, grouped[e][:])
            y_banks[e] = small.tile([N, C], F32, name="y_bank", tag="y_bank")
            columns = slice(e * N, (e + 1) * N)
            nc.tensor.matmul_mx(out=y_banks[e][:],
                                lhsT=w2_words[:, columns].bitcast(FP8X4), lhsT_scale=w2_scales[:, columns],
                                rhs=words.bitcast(FP8X4), rhs_scale=scales, start=True, stop=True)

        def scatter(e):
            place = (e + 1) % 2
            y = sigs[min(e + 1, last)][:].rearrange("s u p b -> s (u p b)")[:, place * C:(place + 1) * C]
            copy_out_of_bank(e)(y, y_banks[e][:])
            nc.vector.tensor_tensor(result[:].indirect(offsets[:, e * LIST_COLS:(e + 1) * LIST_COLS]),
                                    y, gate_wide[:, e * C:(e + 1) * C], MULT)

        nc.sync.dma_start(offsets[:], offs)
        nc.sync.dma_start(token_words[:], x_words.rearrange("o p t r -> p o (t r)").bitcast(I32))
        load(pieces[0])
        for q in range(P // QUADRANT):
            nc.sync.dma_start(token_scales[QUADRANT * q:QUADRANT * q + SCALE_ROWS * PASSES, :].bitcast(I32),
                              x_scales[:, SCALE_ROWS * q:SCALE_ROWS * (q + 1), :].bitcast(I32))
        load(pieces[1])
        nc.sync.dma_start(gate_rows[:], gate[0].rearrange("(p f) -> p f", f=PACK))
        nc.sync.dma_start(w2_raw[:], w2.rearrange("e (p j) n -> p e j n", j=PACK))
        for piece in pieces[2:LOAD_AHEAD]:
            load(piece)

        for o in range(PASSES):
            nc.vector.tensor_copy(slot_words[:, o, :], token_words[:, o, :].bitcast(U32).indirect(offsets[:]))
        nc.vector.tensor_copy(slot_scales[:], token_scales[:].indirect(offsets[:]))

        gate_bank = small.tile([P, PACK, P], F32, name="gate_bank", tag="turned")
        for f in range(PACK):
            nc.tensor.transpose(gate_bank[:, f, :], gate_rows[:, f:f + 1].to_broadcast([P, P]), ident[:])
        nc.scalar.copy(gate_wide[:].rearrange("n (p f) -> n p f", f=PACK), gate_bank[:].rearrange("n f p -> n p f"))

        w2_rounded = work.tile([P, E * N, PACK], BF16, name="w2_rounded", tag="rounded", align_bytes=64)
        for e in range(E):
            round_columns(nc.scalar.copy, w2_rounded[:, e * N:(e + 1) * N, :], w2_raw[:, e, :, :])
        quantise(w2_words[:], w2_scales[:], w2_rounded[:].rearrange("p c j -> p (c j)"))

        steady = len(pieces) - 3
        for index, piece in enumerate(pieces[:steady]):
            kind, e, o, c0, c1 = piece
            if index + LOAD_AHEAD < len(pieces):
                load(pieces[index + LOAD_AHEAD])
            values = round_shared(raw[piece], H, scalar_columns(piece))
            if kind == "w3" and o == 0:
                sigmoid(e)
            if kind == "w1" and e > 0:
                if o == 0:
                    hidden[e - 1] = tail.tile([C, H], BF16, name="hidden", tag="hidden")[:]
                    gated(e - 1, 0, H)
                    if e > 1:
                        scatter(e - 2)
                    turn_hidden(e - 1)
                if o == 1:
                    second_layer(e - 1)
            words, scales = new_codes(coded, H, "first")
            quantise(words, scales, values)
            for a, b in ((0, HALF), (HALF, H)) if (kind, e) == ("w3", last) else ((0, H),):
                multiply(kind, e, o, a, b, words[:, a:b], scales[:, a:b])

        whole, first_half, second_half = pieces[steady:]
        low = round_shared(raw[whole][:, :, 0:HALF], HALF, HALF)
        high = round_shared(raw[whole][:, :, HALF:H], HALF, 0)
        for values, a, b in ((high, HALF, H), (low, 0, HALF)):
            words, scales = new_codes(coded, HALF, "first")
            quantise(words, scales, values)
            multiply("w3", last, PASSES - 2, a, b, words, scales)
        for piece in (first_half, second_half):
            values = round_shared(raw[piece], HALF, scalar_columns(piece))
            words, scales = new_codes(coded, HALF, "first")
            quantise(words, scales, values)
            multiply(*piece, words, scales)
        hidden[last] = values[:, 0:H]
        gated(last, 0, HALF)
        gated(last, HALF, H)
        scatter(last - 1)
        turn_hidden(last)
        second_layer(last)
        scatter(last)
        nc.sync.dma_start(out, result[:])
